import numpy as np
import ml_dtypes


def mxq(x, axis, fmt="e4m3"):
    dtype, down = {"e4m3": (ml_dtypes.float8_e4m3fn, 7), "e5m2": (ml_dtypes.float8_e5m2, 14)}[fmt]
    v = np.moveaxis(np.asarray(x, np.float32).astype(ml_dtypes.bfloat16).astype(np.float64), axis, -1)
    blocks = v.reshape(v.shape[:-1] + (-1, 32))
    amax = np.abs(blocks).max(-1, keepdims=True)
    byte = np.maximum(np.where(amax > 0, np.frexp(amax)[1] - 1 + 127, 0) - down, 1)
    scale = np.exp2(byte - 127.0)
    codes = (blocks / scale).astype(np.float32).astype(dtype).astype(np.float64)
    return np.moveaxis((codes * scale).reshape(v.shape), -1, axis)


WIDE = False


def mx_kscale(k):
    if not WIDE:
        return np.ones(k)
    levels = np.array([10, -10, 5, -5, 0])
    if k % 512:
        return np.exp2(np.random.permutation(np.resize(levels, k // 32))).repeat(32)
    a = np.empty((k // 512, 16))
    for p in range(k // 512):
        a[p, :8] = np.random.permutation(np.resize(levels, 8))
        for g in range(8):
            far = levels[np.abs(levels - a[p, g]) >= 10]
            a[p, g + 8] = far[np.random.randint(len(far))]
    return np.exp2(a.ravel()).repeat(32)


def f64(x):
    return np.asarray(x).astype(np.float64)


def striped(idx):
    return np.tile(idx.reshape(-1, 16).T, (8, 1)).astype(np.uint16)


def unstriped(offs):
    return offs[:16].T.reshape(-1).astype(np.int64)


E2M1 = np.array([0.0, 0.5, 1.0, 1.5, 2.0, 3.0, 4.0, 6.0, -0.0, -0.5, -1.0, -1.5, -2.0, -3.0, -4.0, -6.0])


def pack_weight(w, fmt):
    k, n = w.shape
    w = f64(np.asarray(w, np.float32).astype(ml_dtypes.bfloat16)).reshape(k // 32, 32, n)
    amax = np.abs(w).max(1)
    if fmt == "e4m3":
        byte = np.frexp(amax)[1] - 1 + 127 - 7
    else:
        mant, ex = np.frexp(amax / 6.0)
        byte = np.where(mant > 0.5, ex, ex - 1) + 127
    byte = np.clip(np.where(amax > 0, byte, 1), 1, 254)
    scaled = (w * np.exp2(127.0 - byte)[:, None, :]).reshape(k, n).astype(np.float32)
    by_word = np.ascontiguousarray(scaled.reshape(k // 512, 128, 4, n).transpose(0, 1, 3, 2))
    if fmt == "e4m3":
        words = by_word.astype(ml_dtypes.float8_e4m3fn).view(np.uint8)
    else:
        c = by_word.astype(ml_dtypes.float4_e2m1fn).view(np.uint8) & 0xF
        words = (c[..., 0::2] | (c[..., 1::2] << 4)).reshape(k // 512, 128, 2 * n)
    return np.ascontiguousarray(words), np.ascontiguousarray(byte.astype(np.uint8).reshape(k // 512, 16, n))


def unpack_weight(words, scales, fmt):
    g, _, n = scales.shape
    words = np.ascontiguousarray(words).reshape(g, 128, n, -1)
    if fmt == "e4m3":
        vals = words.view(ml_dtypes.float8_e4m3fn).astype(np.float64)
    else:
        nib = np.empty((g, 128, n, 4), np.uint8)
        nib[..., 0::2] = words & 0xF
        nib[..., 1::2] = words >> 4
        vals = E2M1[nib]
    vals = vals * np.repeat(np.exp2(scales.astype(np.float64) - 127.0), 8, axis=1)[..., None]
    return vals.transpose(0, 1, 3, 2).reshape(g * 512, n)


def relu(v):
    return np.maximum(v, 0.0)


K, T, E, C, H, N = 512, 640, 6, 128, 512, 384
TOP = 3
PAD = 64


def by_expert(wq, xq):
    return np.concatenate([wq[e].T @ xq[:, e * C:(e + 1) * C] for e in range(E)], axis=1)


def setup_inputs():
    n = np.random.standard_normal
    s = mx_kscale(K)[:, None]
    u = mx_kscale(H)
    slot_token = np.empty(E * C, np.int64); pos = np.tile(E * C + np.arange(T) % PAD, (TOP, 1)); taken = np.zeros(T, np.int64)
    liked = np.random.randn(T)
    for e in np.random.permutation(E):
        free = np.flatnonzero(taken < TOP); pick = np.random.permutation(free[np.argsort(-(liked[free] + np.random.gumbel(size=free.size)))[:C]]); slot_token[e * C:(e + 1) * C] = pick
        pos[taken[pick], pick] = e * C + np.arange(C); taken[pick] += 1
    g = np.random.uniform(0.2, 0.8, (TOP, T))
    w1 = [pack_weight(m, "e2m1") for m in n((E, K, H)) / np.sqrt(K) / s[None]]
    w3 = [pack_weight(m, "e2m1") for m in n((E, K, H)) / np.sqrt(K) / s[None] * u[None, None, :]]
    w2 = [pack_weight(m, "e2m1") for m in n((E, H, N)) / np.sqrt(H) / u[None, :, None]]
    return {
        "xT": (n((K, T)) * s).astype(np.float32),
        "w1_words": np.stack([m[0] for m in w1]),
        "w1_scales": np.stack([m[1] for m in w1]),
        "w3_words": np.stack([m[0] for m in w3]),
        "w3_scales": np.stack([m[1] for m in w3]),
        "w2_words": np.stack([m[0] for m in w2]),
        "w2_scales": np.stack([m[1] for m in w2]),
        "gate": np.stack([np.tile(r, (N, 1)) for r in g]).astype(np.float32),
        "offs": striped(slot_token),
        "pos1": striped(pos[0]),
        "pos2": striped(pos[1]),
        "pos3": striped(pos[2]),
    }


def reference(xT, w1_words, w1_scales, w3_words, w3_scales, w2_words, w2_scales, gate, offs, pos1, pos2, pos3):
    idx = unstriped(offs)
    w1 = np.stack([unpack_weight(w1_words[e], w1_scales[e], "e2m1") for e in range(E)])
    w3 = np.stack([unpack_weight(w3_words[e], w3_scales[e], "e2m1") for e in range(E)])
    w2 = np.stack([unpack_weight(w2_words[e], w2_scales[e], "e2m1") for e in range(E)])
    xq = mxq(f64(xT)[:, idx], 0, "e4m3")
    h = relu(by_expert(w1, xq))
    h = h * by_expert(w3, xq)
    y = by_expert(w2, mxq(h, 0, "e4m3"))
    y = np.concatenate([y, np.zeros((N, PAD))], axis=1)
    return sum(f64(gate[r]) * y[:, unstriped(p)] for r, p in enumerate((pos1, pos2, pos3)))

@@ -1,0 +1,252 @@
+from contextlib import ExitStack
+
+import concourse.mybir as mybir
+from concourse.masks import make_identity
+
+K, T, E, C, H, N = 512, 640, 6, 128, 512, 384
+TOP = 3
+PAD = 64
+S = E * C
+FLOPS = 2 * S * (2 * K * H + H * N)
+
+F32 = mybir.dt.float32
+BF16 = mybir.dt.bfloat16
+I32 = mybir.dt.int32
+U32 = mybir.dt.uint32
+U16 = mybir.dt.uint16
+U8 = mybir.dt.uint8
+FP8X4 = mybir.dt.float8_e4m3fn_x4
+FP4X4 = mybir.dt.float4_e2m1fn_x4
+COPY = mybir.ActivationFunctionType.Copy
+RELU = mybir.ActivationFunctionType.Relu
+MULT = mybir.AluOpType.mult
+ADD = mybir.AluOpType.add
+
+P = 128
+NB = N // P
+TOKEN_CHUNKS = ((0, 256), (256, 512), (512, 640))
+SCALE_GROUPS = ((0, 2), (2, 6))
+WORD_GROUPS = ((0, 2), (2, 4), (4, 6))
+GATHER_GROUPS = ((0, 1), (1, 2), (2, 4), (4, 6))
+
+
+def group_of(groups, e):
+    for g, (lo, hi) in enumerate(groups):
+        if lo <= e < hi:
+            return g, e - lo
+    raise ValueError(e)
+
+
+def tile_moe_ecr_glu_relu_kernel(
+    tc, xT, w1_words, w1_scales, w3_words, w3_scales, w2_words, w2_scales, gate, offs, pos1, pos2, pos3, out
+):
+    nc = tc.nc
+    with ExitStack() as ctx:
+        keep = ctx.enter_context(tc.tile_pool(name="keep", bufs=1))
+        work = ctx.enter_context(tc.tile_pool(name="work", bufs=2))
+        psum = ctx.enter_context(tc.psum_pool(name="psum", bufs=1))
+
+        def bank(b, name):
+            return psum.tile([P, 512], F32, name=name, tag="bank%d" % b)
+
+        def plane(name, experts, width):
+            t = keep.tile([P, experts, width], U8, name=name, align_bytes=64)
+            nc.vector.memset(t[:].bitcast(I32), 0)
+            return t
+
+        def load_plane(t, scales, lo, hi):
+            rows = scales.rearrange("e s (q r) n -> r q (e s) n", r=4)
+            for r in range(4):
+                nc.sync.dma_start(t[:].bitcast(I32)[r:P:32], rows[r][:, lo:hi, :].bitcast(I32))
+
+        def load_words(name, words, lo, hi):
+            t = keep.tile([P, hi - lo, words.shape[3]], U8, name=name, align_bytes=64)
+            nc.sync.dma_start(t[:].bitcast(I32), words.rearrange("e s p n -> p (e s) n")[:, lo:hi, :].bitcast(I32))
+            return t
+
+        def load_list(name, src):
+            t = keep.tile([P, src.shape[1]], U16, name=name)
+            nc.sync.dma_start(t[:], src)
+            return t
+
+        s1 = [plane("s1_%d" % g, hi - lo, H) for g, (lo, hi) in enumerate(SCALE_GROUPS[:1])]
+        s3 = [plane("s3_%d" % g, hi - lo, H) for g, (lo, hi) in enumerate(SCALE_GROUPS[:1])]
+        ysb = [keep.tile([P, S + PAD], F32, name="ysb%d" % nb) for nb in range(NB)]
+        nc.vector.memset(ysb[0][:, S:], 0.0)
+        for nb in range(1, NB):
+            nc.scalar.activation(ysb[nb][:, S:], ysb[0][:, S:], RELU)
+        s1.append(plane("s1_1", 4, H))
+        s3.append(plane("s3_1", 4, H))
+        s2 = plane("s2", E, N)
+        x_words = keep.tile([P, T], U32, name="x_words", align_bytes=64)
+        x_scales = keep.tile([P, T], U8, name="x_scales", align_bytes=64)
+        nc.vector.memset(x_scales[:].bitcast(I32), 0)
+        ident = keep.tile([P, P], F32, name="ident")
+        make_identity(nc, ident[:])
+
+        offs_t = load_list("offs_t", offs)
+        x_rows = xT.rearrange("(p j) t -> p j t", j=4)
+        raw = []
+        for c, (lo, hi) in enumerate(TOKEN_CHUNKS):
+            t = keep.tile([P, 4, hi - lo], F32, name="raw%d" % c)
+            nc.sync.dma_start(t[:], x_rows[:, :, lo:hi])
+            raw.append(t)
+        w1 = [load_words("w1_0", w1_words, 0, 2)]
+        w3 = [load_words("w3_0", w3_words, 0, 2)]
+        load_plane(s1[0], w1_scales, 0, 2)
+        load_plane(s3[0], w3_scales, 0, 2)
+        w1.append(load_words("w1_1", w1_words, 2, 4))
+        w3.append(load_words("w3_1", w3_words, 2, 4))
+        load_plane(s1[1], w1_scales, 2, 6)
+        load_plane(s3[1], w3_scales, 2, 6)
+        w1.append(load_words("w1_2", w1_words, 4, 6))
+        w3.append(load_words("w3_2", w3_words, 4, 6))
+        w2 = load_words("w2", w2_words, 0, E)
+        load_plane(s2, w2_scales, 0, E)
+        pos = [load_list("pos%d" % r, src) for r, src in enumerate((pos1, pos2, pos3))]
+        gates = []
+        for nb in range(NB):
+            t = keep.tile([P, TOP, T], F32, name="gate%d" % nb)
+            nc.sync.dma_start(t[:], gate[:, nb * P : (nb + 1) * P, :].rearrange("r n t -> n r t"))
+            gates.append(t)
+
+        for c, (lo, hi) in enumerate(TOKEN_CHUNKS):
+            width = hi - lo
+            grouped = keep.tile([P, width, 4], BF16, name="grouped%d" % c, align_bytes=64)
+            src = raw[c][:].rearrange("p j t -> p t j")
+            if c == 1:
+                nc.scalar.activation(grouped[:, :128, :], src[:, :128, :], COPY)
+                nc.vector.tensor_copy(grouped[:, 128:, :], src[:, 128:, :])
+            else:
+                nc.vector.tensor_copy(grouped[:], src)
+            nc.vector.quantize_mx(
+                out=x_words[:, lo:hi].bitcast(FP8X4),
+                scales=x_scales[:, lo:hi],
+                in_=grouped[:].rearrange("p t j -> p (t j)"),
+            )
+
+        slot_words, slot_scales = [], []
+
+        def gather_tokens(g):
+            lo, hi = GATHER_GROUPS[g]
+            words = keep.tile([P, (hi - lo) * C], U32, name="slot_words%d" % g, align_bytes=64)
+            scales = keep.tile([P, (hi - lo) * C], U8, name="slot_scales%d" % g, align_bytes=64)
+            part = offs_t[:, lo * C // 16 : hi * C // 16]
+            nc.vector.tensor_copy(words[:], x_words[:].indirect(part))
+            nc.vector.tensor_copy(scales[:], x_scales[:].indirect(part))
+            slot_words.append(words)
+            slot_scales.append(scales)
+
+        h_words = keep.tile([P, S], U32, name="h_words", align_bytes=64)
+        h_scales = keep.tile([P, S], U8, name="h_scales", align_bytes=64)
+
+        def first_layer(e):
+            g, j = group_of(GATHER_GROUPS, e)
+            gw, jw = group_of(WORD_GROUPS, e)
+            gs, js = group_of(SCALE_GROUPS, e)
+            cols = slice(j * C, (j + 1) * C)
+            a = bank(e % 2, "a%d" % e)
+            b = bank(2 + e % 2, "b%d" % e)
+            for acc, words, scales in ((a, w1, s1), (b, w3, s3)):
+                nc.tensor.matmul_mx(
+                    out=acc[:],
+                    lhsT=slot_words[g][:, cols].bitcast(FP8X4),
+                    lhsT_scale=slot_scales[g][:, cols],
+                    rhs=words[gw][:, jw, :].bitcast(FP4X4),
+                    rhs_scale=scales[gs][:, js, :],
+                    start=True,
+                    stop=True,
+                )
+            relu_a = work.tile([P, 2, P, 2], F32, name="relu_a")
+            nc.scalar.activation(relu_a[:], a[:].rearrange("s (p u d) -> s u p d", u=2, d=2), RELU)
+            h = work.tile([P, 2, P, 2], BF16, name="h")
+            nc.vector.tensor_tensor(h[:], b[:].rearrange("s (p u d) -> s u p d", u=2, d=2), relu_a[:], MULT)
+            return h
+
+        def turn_and_quantise(e, h):
+            pairs = h[:].rearrange("s u p d -> s (u p d)").bitcast(F32)
+            turned = bank(4 + e % 2, "turned%d" % e)
+            for u in range(2):
+                nc.tensor.transpose(turned[:, u * C : (u + 1) * C], pairs[:, u * P : (u + 1) * P], ident[:])
+            h_grouped = work.tile([P, C * 4], BF16, name="h_grouped", align_bytes=64)
+            nc.scalar.copy(
+                h_grouped[:].bitcast(F32).rearrange("p (s u) -> p s u", u=2),
+                turned[:, : 2 * C].rearrange("p (u s) -> p s u", u=2),
+            )
+            cols = slice(e * C, (e + 1) * C)
+            nc.vector.quantize_mx(out=h_words[:, cols].bitcast(FP8X4), scales=h_scales[:, cols], in_=h_grouped[:])
+
+        def second_layer(acc, nb, e, first):
+            cols = slice(e * C, (e + 1) * C)
+            nc.tensor.matmul_mx(
+                out=acc[:, (e - first) * C : (e - first + 1) * C],
+                lhsT=w2[:, e, nb * 2 * P : (nb + 1) * 2 * P].bitcast(FP4X4),
+                lhsT_scale=s2[:, e, nb * P : (nb + 1) * P],
+                rhs=h_words[:, cols].bitcast(FP8X4),
+                rhs_scale=h_scales[:, cols],
+                start=True,
+                stop=True,
+            )
+
+        def copy_out(acc, nb, lo, hi):
+            nc.scalar.copy(ysb[nb][:, lo * C : hi * C], acc[:, : (hi - lo) * C])
+
+        gather_tokens(0)
+        gather_tokens(1)
+        acc = bank(6, "y0_head")
+        hs = {0: first_layer(0)}
+        for e in range(E):
+            if e == 0:
+                gather_tokens(2)
+            if e == 2:
+                gather_tokens(3)
+            if e + 1 < E:
+                hs[e + 1] = first_layer(e + 1)
+            turn_and_quantise(e, hs[e])
+            if e < 4:
+                second_layer(acc, 0, e, 0)
+                if e == 3:
+                    copy_out(acc, 0, 0, 4)
+            else:
+                acc = bank(7 if e == 4 else 6, "y0_%d" % e)
+                second_layer(acc, 0, e, e)
+                copy_out(acc, 0, e, e + 1)
+        for nb in range(1, NB):
+            for b, lo, hi in ((5, 2, 6), (6, 0, 2)):
+                acc = bank(b, "y%d_%d" % (nb, lo))
+                for e in range(lo, hi):
+                    second_layer(acc, nb, e, lo)
+                copy_out(acc, nb, lo, hi)
+
+        def turn(dst, srcs):
+            for i, src in enumerate(srcs):
+                nc.tensor.matmul(dst, src, ident[:], start=(i == 0), stop=(i == len(srcs) - 1), is_transpose=True)
+
+        for nb in range(NB):
+            prods = []
+            for r in range(TOP):
+                t = work.tile([P, T], F32, name="prod%d" % r)
+                nc.vector.tensor_tensor(t[:], ysb[nb][:].indirect(pos[r][:]), gates[nb][:, r, :], MULT)
+                prods.append(t)
+            total = work.tile([P, T], F32, name="total")
+            if nb + 1 < NB:
+                summed = work.tile([P, T], F32, name="summed")
+                for b, lo, hi in ((0, 0, 4), (1, 4, 5)):
+                    acc = bank(b, "sum%d_%d" % (nb, lo))
+                    for c in range(lo, hi):
+                        turn(acc[:, (c - lo) * P : (c - lo + 1) * P], [t[:, c * P : (c + 1) * P] for t in prods])
+                    nc.scalar.copy(summed[:, lo * P : hi * P], acc[:, : (hi - lo) * P])
+                for b, lo, hi in ((2, 0, 4), (3, 4, 5)):
+                    acc = bank(b, "back%d_%d" % (nb, lo))
+                    for c in range(lo, hi):
+                        turn(acc[:, (c - lo) * P : (c - lo + 1) * P], [summed[:, c * P : (c + 1) * P]])
+                    nc.scalar.copy(total[:, lo * P : hi * P], acc[:, : (hi - lo) * P])
+                nc.sync.dma_start(out[nb * P : (nb + 1) * P, :], total[:])
+            else:
+                part = work.tile([P, T], F32, name="part")
+                halves = ((0, T // 2), (T // 2, T))
+                for lo, hi in halves:
+                    nc.vector.tensor_tensor(part[:, lo:hi], prods[0][:, lo:hi], prods[1][:, lo:hi], ADD)
+                for lo, hi in halves:
+                    nc.vector.tensor_tensor(total[:, lo:hi], part[:, lo:hi], prods[2][:, lo:hi], ADD)
+                    nc.sync.dma_start(out[nb * P : (nb + 1) * P, lo:hi], total[:, lo:hi])

@@ -25,7 +25,6 @@ ADD = mybir.AluOpType.add
 P = 128
 NB = N // P
 TOKEN_CHUNKS = ((0, 256), (256, 512), (512, 640))
-SCALE_GROUPS = ((0, 2), (2, 6))
 WORD_GROUPS = ((0, 2), (2, 4), (4, 6))
 GATHER_GROUPS = ((0, 1), (1, 2), (2, 4), (4, 6))
 
@@ -69,38 +68,33 @@ def tile_moe_ecr_glu_relu_kernel(
             nc.sync.dma_start(t[:], src)
             return t
 
-        s1 = [plane("s1_%d" % g, hi - lo, H) for g, (lo, hi) in enumerate(SCALE_GROUPS[:1])]
-        s3 = [plane("s3_%d" % g, hi - lo, H) for g, (lo, hi) in enumerate(SCALE_GROUPS[:1])]
+        s1 = plane("s1", E, H)
         ysb = [keep.tile([P, S + PAD], F32, name="ysb%d" % nb) for nb in range(NB)]
         nc.vector.memset(ysb[0][:, S:], 0.0)
         for nb in range(1, NB):
             nc.scalar.activation(ysb[nb][:, S:], ysb[0][:, S:], RELU)
-        s1.append(plane("s1_1", 4, H))
-        s3.append(plane("s3_1", 4, H))
-        s2 = plane("s2", E, N)
+        s3 = plane("s3", E, H)
         x_words = keep.tile([P, T], U32, name="x_words", align_bytes=64)
         x_scales = keep.tile([P, T], U8, name="x_scales", align_bytes=64)
         nc.vector.memset(x_scales[:].bitcast(I32), 0)
+        s2 = plane("s2", E, N)
         ident = keep.tile([P, P], F32, name="ident")
         make_identity(nc, ident[:])
 
-        offs_t = load_list("offs_t", offs)
         x_rows = xT.rearrange("(p j) t -> p j t", j=4)
         raw = []
         for c, (lo, hi) in enumerate(TOKEN_CHUNKS):
             t = keep.tile([P, 4, hi - lo], F32, name="raw%d" % c)
             nc.sync.dma_start(t[:], x_rows[:, :, lo:hi])
             raw.append(t)
-        w1 = [load_words("w1_0", w1_words, 0, 2)]
-        w3 = [load_words("w3_0", w3_words, 0, 2)]
-        load_plane(s1[0], w1_scales, 0, 2)
-        load_plane(s3[0], w3_scales, 0, 2)
-        w1.append(load_words("w1_1", w1_words, 2, 4))
-        w3.append(load_words("w3_1", w3_words, 2, 4))
-        load_plane(s1[1], w1_scales, 2, 6)
-        load_plane(s3[1], w3_scales, 2, 6)
-        w1.append(load_words("w1_2", w1_words, 4, 6))
-        w3.append(load_words("w3_2", w3_words, 4, 6))
+        offs_t = load_list("offs_t", offs)
+        load_plane(s1, w1_scales, 0, E)
+        w1, w3 = [], []
+        for g, (lo, hi) in enumerate(WORD_GROUPS):
+            w1.append(load_words("w1_%d" % g, w1_words, lo, hi))
+            w3.append(load_words("w3_%d" % g, w3_words, lo, hi))
+            if g == 0:
+                load_plane(s3, w3_scales, 0, E)
         w2 = load_words("w2", w2_words, 0, E)
         load_plane(s2, w2_scales, 0, E)
         pos = [load_list("pos%d" % r, src) for r, src in enumerate((pos1, pos2, pos3))]
@@ -143,7 +137,6 @@ def tile_moe_ecr_glu_relu_kernel(
         def first_layer(e):
             g, j = group_of(GATHER_GROUPS, e)
             gw, jw = group_of(WORD_GROUPS, e)
-            gs, js = group_of(SCALE_GROUPS, e)
             cols = slice(j * C, (j + 1) * C)
             a = bank(e % 2, "a%d" % e)
             b = bank(2 + e % 2, "b%d" % e)
@@ -153,7 +146,7 @@ def tile_moe_ecr_glu_relu_kernel(
                     lhsT=slot_words[g][:, cols].bitcast(FP8X4),
                     lhsT_scale=slot_scales[g][:, cols],
                     rhs=words[gw][:, jw, :].bitcast(FP4X4),
-                    rhs_scale=scales[gs][:, js, :],
+                    rhs_scale=scales[:, e, :],
                     start=True,
                     stop=True,
                 )

@@ -101,7 +101,9 @@ def tile_moe_ecr_glu_relu_kernel(
         gates = []
         for nb in range(NB):
             t = keep.tile([P, TOP, T], F32, name="gate%d" % nb)
-            nc.sync.dma_start(t[:], gate[:, nb * P : (nb + 1) * P, :].rearrange("r n t -> n r t"))
+            rows = gate[:, nb * P : (nb + 1) * P, :].rearrange("r n t -> n r t")
+            for lo, hi in ((0, 1), (1, 2), (2, 3)) if nb == 0 else ((0, TOP),):
+                nc.sync.dma_start(t[:, lo:hi, :], rows[:, lo:hi, :])
             gates.append(t)
 
         for c, (lo, hi) in enumerate(TOKEN_CHUNKS):
@@ -134,112 +136,142 @@ def tile_moe_ecr_glu_relu_kernel(
         h_words = keep.tile([P, S], U32, name="h_words", align_bytes=64)
         h_scales = keep.tile([P, S], U8, name="h_scales", align_bytes=64)
 
-        def first_layer(e):
+        def first_layer(b, name, words, scales, e):
             g, j = group_of(GATHER_GROUPS, e)
             gw, jw = group_of(WORD_GROUPS, e)
             cols = slice(j * C, (j + 1) * C)
-            a = bank(e % 2, "a%d" % e)
-            b = bank(2 + e % 2, "b%d" % e)
-            for acc, words, scales in ((a, w1, s1), (b, w3, s3)):
-                nc.tensor.matmul_mx(
-                    out=acc[:],
-                    lhsT=slot_words[g][:, cols].bitcast(FP8X4),
-                    lhsT_scale=slot_scales[g][:, cols],
-                    rhs=words[gw][:, jw, :].bitcast(FP4X4),
-                    rhs_scale=scales[:, e, :],
-                    start=True,
-                    stop=True,
-                )
-            relu_a = work.tile([P, 2, P, 2], F32, name="relu_a")
-            nc.scalar.activation(relu_a[:], a[:].rearrange("s (p u d) -> s u p d", u=2, d=2), RELU)
-            h = work.tile([P, 2, P, 2], BF16, name="h")
-            nc.vector.tensor_tensor(h[:], b[:].rearrange("s (p u d) -> s u p d", u=2, d=2), relu_a[:], MULT)
-            return h
-
-        def turn_and_quantise(e, h):
-            pairs = h[:].rearrange("s u p d -> s (u p d)").bitcast(F32)
-            turned = bank(4 + e % 2, "turned%d" % e)
-            for u in range(2):
-                nc.tensor.transpose(turned[:, u * C : (u + 1) * C], pairs[:, u * P : (u + 1) * P], ident[:])
-            h_grouped = work.tile([P, C * 4], BF16, name="h_grouped", align_bytes=64)
-            nc.scalar.copy(
-                h_grouped[:].bitcast(F32).rearrange("p (s u) -> p s u", u=2),
-                turned[:, : 2 * C].rearrange("p (u s) -> p s u", u=2),
-            )
-            cols = slice(e * C, (e + 1) * C)
-            nc.vector.quantize_mx(out=h_words[:, cols].bitcast(FP8X4), scales=h_scales[:, cols], in_=h_grouped[:])
-
-        def second_layer(acc, nb, e, first):
-            cols = slice(e * C, (e + 1) * C)
+            acc = bank(b, "%s%d" % (name, e))
             nc.tensor.matmul_mx(
-                out=acc[:, (e - first) * C : (e - first + 1) * C],
-                lhsT=w2[:, e, nb * 2 * P : (nb + 1) * 2 * P].bitcast(FP4X4),
-                lhsT_scale=s2[:, e, nb * P : (nb + 1) * P],
-                rhs=h_words[:, cols].bitcast(FP8X4),
-                rhs_scale=h_scales[:, cols],
+                out=acc[:],
+                lhsT=slot_words[g][:, cols].bitcast(FP8X4),
+                lhsT_scale=slot_scales[g][:, cols],
+                rhs=words[gw][:, jw, :].bitcast(FP4X4),
+                rhs_scale=scales[:, e, :],
                 start=True,
                 stop=True,
             )
+            return acc[:].rearrange("s (p u d) -> s u p d", u=2, d=2)
 
-        def copy_out(acc, nb, lo, hi):
+        def gate_side(e):
+            relu_a = work.tile([P, 2, P, 2], F32, name="relu_a", bufs=E)
+            nc.scalar.activation(relu_a[:], first_layer(e % 2, "a", w1, s1, e), RELU)
+            return relu_a
+
+        def value_side(e):
+            return first_layer(2 + e % 3, "b", w3, s3, e)
+
+        def hidden(relu_a, b):
+            h = work.tile([P, 2, P, 2], BF16, name="h", bufs=E)
+            nc.vector.tensor_tensor(h[:], b, relu_a[:], MULT)
+            return h
+
+        h_grouped = keep.tile([P, S * 4], BF16, name="h_grouped", align_bytes=64)
+
+        def turn(dst, src, start=True, stop=True):
+            nc.tensor.matmul(dst, src, ident[:], start=start, stop=stop, is_transpose=True)
+
+        def turn_hidden(e, h):
+            pairs = h[:].rearrange("s u p d -> s (u p d)").bitcast(F32)
+            turned = bank(5 + e % 2, "turned%d" % e)
+            for u in range(2):
+                turn(turned[:, u * C : (u + 1) * C], pairs[:, u * P : (u + 1) * P])
+            nc.scalar.copy(
+                h_grouped[:, e * 4 * C : (e + 1) * 4 * C].bitcast(F32).rearrange("p (s u) -> p s u", u=2),
+                turned[:, : 2 * C].rearrange("p (u s) -> p s u", u=2),
+            )
+
+        def quantise_hidden(lo, hi):
+            cols = slice(lo * C, hi * C)
+            nc.vector.quantize_mx(
+                out=h_words[:, cols].bitcast(FP8X4), scales=h_scales[:, cols], in_=h_grouped[:, lo * 4 * C : hi * 4 * C]
+            )
+
+        def second_layer(b, nb, lo, hi):
+            acc = bank(b, "y%d_%d" % (nb, lo))
+            for e in range(lo, hi):
+                cols = slice(e * C, (e + 1) * C)
+                nc.tensor.matmul_mx(
+                    out=acc[:, (e - lo) * C : (e - lo + 1) * C],
+                    lhsT=w2[:, e, nb * 2 * P : (nb + 1) * 2 * P].bitcast(FP4X4),
+                    lhsT_scale=s2[:, e, nb * P : (nb + 1) * P],
+                    rhs=h_words[:, cols].bitcast(FP8X4),
+                    rhs_scale=h_scales[:, cols],
+                    start=True,
+                    stop=True,
+                )
             nc.scalar.copy(ysb[nb][:, lo * C : hi * C], acc[:, : (hi - lo) * C])
 
-        gather_tokens(0)
-        gather_tokens(1)
-        acc = bank(6, "y0_head")
-        hs = {0: first_layer(0)}
+        for g in range(len(GATHER_GROUPS)):
+            gather_tokens(g)
+        relus, values, hs = [], [], []
         for e in range(E):
-            if e == 0:
-                gather_tokens(2)
-            if e == 2:
-                gather_tokens(3)
-            if e + 1 < E:
-                hs[e + 1] = first_layer(e + 1)
-            turn_and_quantise(e, hs[e])
-            if e < 4:
-                second_layer(acc, 0, e, 0)
-                if e == 3:
-                    copy_out(acc, 0, 0, 4)
-            else:
-                acc = bank(7 if e == 4 else 6, "y0_%d" % e)
-                second_layer(acc, 0, e, e)
-                copy_out(acc, 0, e, e + 1)
+            relus.append(gate_side(e))
+            if e < 3:
+                values.append(value_side(e))
+        for e in range(E):
+            hs.append(hidden(relus[e], values[e]))
+            if e + 3 < E:
+                values.append(value_side(e + 3))
+            if 1 <= e <= 4:
+                turn_hidden(e - 1, hs[e - 1])
+            if e == 3:
+                quantise_hidden(0, 2)
+        second_layer(2, 0, 0, 2)
+        turn_hidden(4, hs[4])
+        turn_hidden(5, hs[5])
+        quantise_hidden(2, 3)
+        quantise_hidden(3, 5)
+        second_layer(0, 0, 2, 5)
+        quantise_hidden(5, 6)
+        second_layer(1, 0, 5, 6)
         for nb in range(1, NB):
-            for b, lo, hi in ((5, 2, 6), (6, 0, 2)):
-                acc = bank(b, "y%d_%d" % (nb, lo))
-                for e in range(lo, hi):
-                    second_layer(acc, nb, e, lo)
-                copy_out(acc, nb, lo, hi)
+            second_layer(6, nb, 2, 6)
+            second_layer(1, nb, 0, 2)
 
-        def turn(dst, srcs):
-            for i, src in enumerate(srcs):
-                nc.tensor.matmul(dst, src, ident[:], start=(i == 0), stop=(i == len(srcs) - 1), is_transpose=True)
+        def gather_results(nb, r, lo, hi):
+            t = work.tile([P, hi - lo], F32, name="prod%d" % r)
+            part = pos[r][:, lo // 16 : hi // 16]
+            nc.vector.tensor_tensor(t[:], ysb[nb][:].indirect(part), gates[nb][:, r, lo:hi], MULT)
+            return t
 
-        for nb in range(NB):
-            prods = []
+        def combine_on_tensor(nb, lo, hi, pieces):
+            sums = [bank(b, "sum%d_%d" % (nb, c0)) for b, back, c0, c1 in pieces]
             for r in range(TOP):
-                t = work.tile([P, T], F32, name="prod%d" % r)
-                nc.vector.tensor_tensor(t[:], ysb[nb][:].indirect(pos[r][:]), gates[nb][:, r, :], MULT)
-                prods.append(t)
-            total = work.tile([P, T], F32, name="total")
-            if nb + 1 < NB:
-                summed = work.tile([P, T], F32, name="summed")
-                for b, lo, hi in ((0, 0, 4), (1, 4, 5)):
-                    acc = bank(b, "sum%d_%d" % (nb, lo))
-                    for c in range(lo, hi):
-                        turn(acc[:, (c - lo) * P : (c - lo + 1) * P], [t[:, c * P : (c + 1) * P] for t in prods])
-                    nc.scalar.copy(summed[:, lo * P : hi * P], acc[:, : (hi - lo) * P])
-                for b, lo, hi in ((2, 0, 4), (3, 4, 5)):
-                    acc = bank(b, "back%d_%d" % (nb, lo))
-                    for c in range(lo, hi):
-                        turn(acc[:, (c - lo) * P : (c - lo + 1) * P], [summed[:, c * P : (c + 1) * P]])
-                    nc.scalar.copy(total[:, lo * P : hi * P], acc[:, : (hi - lo) * P])
-                nc.sync.dma_start(out[nb * P : (nb + 1) * P, :], total[:])
-            else:
-                part = work.tile([P, T], F32, name="part")
-                halves = ((0, T // 2), (T // 2, T))
-                for lo, hi in halves:
-                    nc.vector.tensor_tensor(part[:, lo:hi], prods[0][:, lo:hi], prods[1][:, lo:hi], ADD)
-                for lo, hi in halves:
-                    nc.vector.tensor_tensor(total[:, lo:hi], part[:, lo:hi], prods[2][:, lo:hi], ADD)
-                    nc.sync.dma_start(out[nb * P : (nb + 1) * P, lo:hi], total[:, lo:hi])
+                t = gather_results(nb, r, lo, hi)
+                for acc, (b, back, c0, c1) in zip(sums, pieces):
+                    for c in range(c0, c1):
+                        turn(
+                            acc[:, (c - c0) * P : (c - c0 + 1) * P],
+                            t[:, c * P : (c + 1) * P],
+                            start=(r == 0 and c == c0),
+                            stop=(r == TOP - 1 and c == c1 - 1),
+                        )
+            summed = work.tile([P, hi - lo], F32, name="summed")
+            total = work.tile([P, hi - lo], F32, name="total")
+            for acc, (b, back, c0, c1) in zip(sums, pieces):
+                nc.scalar.copy(summed[:, c0 * P : c1 * P], acc[:, : (c1 - c0) * P])
+            for b, back, c0, c1 in pieces:
+                acc = bank(back, "back%d_%d" % (nb, c0))
+                for c in range(c0, c1):
+                    turn(acc[:, (c - c0) * P : (c - c0 + 1) * P], summed[:, c * P : (c + 1) * P])
+                nc.scalar.copy(total[:, c0 * P : c1 * P], acc[:, : (c1 - c0) * P])
+            nc.sync.dma_start(out[nb * P : (nb + 1) * P, lo:hi], total[:])
+
+        def combine_on_vector(nb, lo, hi):
+            first = gather_results(nb, 0, lo, hi)
+            second = gather_results(nb, 1, lo, hi)
+            third = gather_results(nb, 2, lo, hi)
+            part = work.tile([P, hi - lo], F32, name="part")
+            last = work.tile([P, hi - lo], F32, name="last")
+            half = (hi - lo) // 2
+            halves = (slice(0, half), slice(half, 2 * half))
+            for cols in halves:
+                nc.vector.tensor_tensor(part[:, cols], first[:, cols], second[:, cols], ADD)
+            for cols in halves:
+                nc.vector.tensor_tensor(last[:, cols], part[:, cols], third[:, cols], ADD)
+                nc.sync.dma_start(out[nb * P : (nb + 1) * P, lo + cols.start : lo + cols.stop], last[:, cols])
+
+        combine_on_tensor(0, 0, T, ((2, 4, 0, 3), (3, 5, 3, 5)))
+        combine_on_tensor(1, 0, T, ((7, 4, 0, 3), (0, 5, 3, 5)))
+        combine_on_tensor(2, 0, 256, ((2, 3, 0, 2),))
+        combine_on_vector(2, 256, T)

@@ -158,7 +158,7 @@ def tile_moe_ecr_glu_relu_kernel(
             return relu_a
 
         def value_side(e):
-            return first_layer(2 + e % 3, "b", w3, s3, e)
+            return first_layer((2, 3, 7, 4, 2, 3)[e], "b", w3, s3, e)
 
         def hidden(relu_a, b):
             h = work.tile([P, 2, P, 2], BF16, name="h", bufs=E)
@@ -170,14 +170,16 @@ def tile_moe_ecr_glu_relu_kernel(
         def turn(dst, src, start=True, stop=True):
             nc.tensor.matmul(dst, src, ident[:], start=start, stop=stop, is_transpose=True)
 
-        def turn_hidden(e, h):
-            pairs = h[:].rearrange("s u p d -> s (u p d)").bitcast(F32)
-            turned = bank(5 + e % 2, "turned%d" % e)
-            for u in range(2):
-                turn(turned[:, u * C : (u + 1) * C], pairs[:, u * P : (u + 1) * P])
-            nc.scalar.copy(
-                h_grouped[:, e * 4 * C : (e + 1) * 4 * C].bitcast(F32).rearrange("p (s u) -> p s u", u=2),
-                turned[:, : 2 * C].rearrange("p (u s) -> p s u", u=2),
+        def turn_hidden(b, lo, hi, copy):
+            turned = bank(b, "turned%d" % lo)
+            for e in range(lo, hi):
+                pairs = hs[e][:].rearrange("s u p d -> s (u p d)").bitcast(F32)
+                for u in range(2):
+                    at = (2 * (e - lo) + u) * C
+                    turn(turned[:, at : at + C], pairs[:, u * P : (u + 1) * P])
+            copy(
+                h_grouped[:, lo * 4 * C : hi * 4 * C].bitcast(F32).rearrange("p (e s u) -> p e s u", u=2, s=C),
+                turned[:, : (hi - lo) * 2 * C].rearrange("p (e u s) -> p e s u", u=2, s=C),
             )
 
         def quantise_hidden(lo, hi):
@@ -186,7 +188,7 @@ def tile_moe_ecr_glu_relu_kernel(
                 out=h_words[:, cols].bitcast(FP8X4), scales=h_scales[:, cols], in_=h_grouped[:, lo * 4 * C : hi * 4 * C]
             )
 
-        def second_layer(b, nb, lo, hi):
+        def second_layer(b, nb, lo, hi, copy=nc.scalar.copy):
             acc = bank(b, "y%d_%d" % (nb, lo))
             for e in range(lo, hi):
                 cols = slice(e * C, (e + 1) * C)
@@ -199,30 +201,32 @@ def tile_moe_ecr_glu_relu_kernel(
                     start=True,
                     stop=True,
                 )
-            nc.scalar.copy(ysb[nb][:, lo * C : hi * C], acc[:, : (hi - lo) * C])
+            copy(ysb[nb][:, lo * C : hi * C], acc[:, : (hi - lo) * C])
 
         for g in range(len(GATHER_GROUPS)):
             gather_tokens(g)
-        relus, values, hs = [], [], []
+        relus, values, hs = {}, {}, {}
         for e in range(E):
-            relus.append(gate_side(e))
-            if e < 3:
-                values.append(value_side(e))
-        for e in range(E):
-            hs.append(hidden(relus[e], values[e]))
-            if e + 3 < E:
-                values.append(value_side(e + 3))
-            if 1 <= e <= 4:
-                turn_hidden(e - 1, hs[e - 1])
-            if e == 3:
-                quantise_hidden(0, 2)
-        second_layer(2, 0, 0, 2)
-        turn_hidden(4, hs[4])
-        turn_hidden(5, hs[5])
-        quantise_hidden(2, 3)
-        quantise_hidden(3, 5)
-        second_layer(0, 0, 2, 5)
+            relus[e] = gate_side(e)
+            if e < 4:
+                values[e] = value_side(e)
+        for e in (0, 1):
+            hs[e] = hidden(relus[e], values[e])
+            values[e + 4] = value_side(e + 4)
+        turn_hidden(5, 0, 2, nc.scalar.copy)
+        for e in (2, 3):
+            hs[e] = hidden(relus[e], values[e])
+        turn_hidden(6, 2, 4, nc.scalar.copy)
+        for e in (4, 5):
+            hs[e] = hidden(relus[e], values[e])
+        turn_hidden(4, 4, 5, nc.vector.tensor_copy)
+        turn_hidden(7, 5, 6, nc.scalar.copy)
+        quantise_hidden(0, 2)
+        quantise_hidden(2, 4)
+        second_layer(0, 0, 0, 4)
+        quantise_hidden(4, 5)
         quantise_hidden(5, 6)
+        second_layer(5, 0, 4, 5, nc.vector.tensor_copy)
         second_layer(1, 0, 5, 6)
         for nb in range(1, NB):
             second_layer(6, nb, 2, 6)

from contextlib import ExitStack

import concourse.mybir as mybir
from concourse.masks import make_identity

K, T, E, C, H, N = 512, 640, 6, 128, 512, 384
TOP = 3
PAD = 64
S = E * C
FLOPS = 2 * S * (2 * K * H + H * N)

F32 = mybir.dt.float32
BF16 = mybir.dt.bfloat16
I32 = mybir.dt.int32
U32 = mybir.dt.uint32
U16 = mybir.dt.uint16
U8 = mybir.dt.uint8
FP8X4 = mybir.dt.float8_e4m3fn_x4
FP4X4 = mybir.dt.float4_e2m1fn_x4
COPY = mybir.ActivationFunctionType.Copy
RELU = mybir.ActivationFunctionType.Relu
MULT = mybir.AluOpType.mult
ADD = mybir.AluOpType.add

P = 128
NB = N // P
TOKEN_CHUNKS = ((0, 256), (256, 512), (512, 640))
WORD_GROUPS = ((0, 2), (2, 4), (4, 6))
GATHER_GROUPS = ((0, 1), (1, 2), (2, 4), (4, 6))


def group_of(groups, e):
    for g, (lo, hi) in enumerate(groups):
        if lo <= e < hi:
            return g, e - lo
    raise ValueError(e)


def tile_moe_ecr_glu_relu_kernel(
    tc, xT, w1_words, w1_scales, w3_words, w3_scales, w2_words, w2_scales, gate, offs, pos1, pos2, pos3, out
):
    nc = tc.nc
    with ExitStack() as ctx:
        keep = ctx.enter_context(tc.tile_pool(name="keep", bufs=1))
        work = ctx.enter_context(tc.tile_pool(name="work", bufs=2))
        psum = ctx.enter_context(tc.psum_pool(name="psum", bufs=1))

        def bank(b, name):
            return psum.tile([P, 512], F32, name=name, tag="bank%d" % b)

        def plane(name, experts, width):
            t = keep.tile([P, experts, width], U8, name=name, align_bytes=64)
            nc.vector.memset(t[:].bitcast(I32), 0)
            return t

        def load_plane(t, scales, lo, hi):
            rows = scales.rearrange("e s (q r) n -> r q (e s) n", r=4)
            for r in range(4):
                nc.sync.dma_start(t[:].bitcast(I32)[r:P:32], rows[r][:, lo:hi, :].bitcast(I32))

        def load_words(name, words, lo, hi):
            t = keep.tile([P, hi - lo, words.shape[3]], U8, name=name, align_bytes=64)
            nc.sync.dma_start(t[:].bitcast(I32), words.rearrange("e s p n -> p (e s) n")[:, lo:hi, :].bitcast(I32))
            return t

        def load_list(name, src):
            t = keep.tile([P, src.shape[1]], U16, name=name)
            nc.sync.dma_start(t[:], src)
            return t

        s1 = plane("s1", E, H)
        ysb = [keep.tile([P, S + PAD], F32, name="ysb%d" % nb) for nb in range(NB)]
        nc.vector.memset(ysb[0][:, S:], 0.0)
        for nb in range(1, NB):
            nc.scalar.activation(ysb[nb][:, S:], ysb[0][:, S:], RELU)
        s3 = plane("s3", E, H)
        x_words = keep.tile([P, T], U32, name="x_words", align_bytes=64)
        x_scales = keep.tile([P, T], U8, name="x_scales", align_bytes=64)
        nc.vector.memset(x_scales[:].bitcast(I32), 0)
        s2 = plane("s2", E, N)
        ident = keep.tile([P, P], F32, name="ident")
        make_identity(nc, ident[:])

        x_rows = xT.rearrange("(p j) t -> p j t", j=4)
        raw = []
        for c, (lo, hi) in enumerate(TOKEN_CHUNKS):
            t = keep.tile([P, 4, hi - lo], F32, name="raw%d" % c)
            nc.sync.dma_start(t[:], x_rows[:, :, lo:hi])
            raw.append(t)
        offs_t = load_list("offs_t", offs)
        load_plane(s1, w1_scales, 0, E)
        w1, w3 = [], []
        for g, (lo, hi) in enumerate(WORD_GROUPS):
            w1.append(load_words("w1_%d" % g, w1_words, lo, hi))
            w3.append(load_words("w3_%d" % g, w3_words, lo, hi))
            if g == 0:
                load_plane(s3, w3_scales, 0, E)
        w2 = load_words("w2", w2_words, 0, E)
        load_plane(s2, w2_scales, 0, E)
        pos = [load_list("pos%d" % r, src) for r, src in enumerate((pos1, pos2, pos3))]
        gates = []
        for nb in range(NB):
            t = keep.tile([P, TOP, T], F32, name="gate%d" % nb)
            rows = gate[:, nb * P : (nb + 1) * P, :].rearrange("r n t -> n r t")
            for lo, hi in ((0, 1), (1, 2), (2, 3)) if nb == 0 else ((0, TOP),):
                nc.sync.dma_start(t[:, lo:hi, :], rows[:, lo:hi, :])
            gates.append(t)

        for c, (lo, hi) in enumerate(TOKEN_CHUNKS):
            width = hi - lo
            grouped = keep.tile([P, width, 4], BF16, name="grouped%d" % c, align_bytes=64)
            src = raw[c][:].rearrange("p j t -> p t j")
            if c == 1:
                nc.scalar.activation(grouped[:, :128, :], src[:, :128, :], COPY)
                nc.vector.tensor_copy(grouped[:, 128:, :], src[:, 128:, :])
            else:
                nc.vector.tensor_copy(grouped[:], src)
            nc.vector.quantize_mx(
                out=x_words[:, lo:hi].bitcast(FP8X4),
                scales=x_scales[:, lo:hi],
                in_=grouped[:].rearrange("p t j -> p (t j)"),
            )

        slot_words, slot_scales = [], []

        def gather_tokens(g):
            lo, hi = GATHER_GROUPS[g]
            words = keep.tile([P, (hi - lo) * C], U32, name="slot_words%d" % g, align_bytes=64)
            scales = keep.tile([P, (hi - lo) * C], U8, name="slot_scales%d" % g, align_bytes=64)
            part = offs_t[:, lo * C // 16 : hi * C // 16]
            nc.vector.tensor_copy(words[:], x_words[:].indirect(part))
            nc.vector.tensor_copy(scales[:], x_scales[:].indirect(part))
            slot_words.append(words)
            slot_scales.append(scales)

        h_words = keep.tile([P, S], U32, name="h_words", align_bytes=64)
        h_scales = keep.tile([P, S], U8, name="h_scales", align_bytes=64)

        def first_layer(b, name, words, scales, e):
            g, j = group_of(GATHER_GROUPS, e)
            gw, jw = group_of(WORD_GROUPS, e)
            cols = slice(j * C, (j + 1) * C)
            acc = bank(b, "%s%d" % (name, e))
            nc.tensor.matmul_mx(
                out=acc[:],
                lhsT=slot_words[g][:, cols].bitcast(FP8X4),
                lhsT_scale=slot_scales[g][:, cols],
                rhs=words[gw][:, jw, :].bitcast(FP4X4),
                rhs_scale=scales[:, e, :],
                start=True,
                stop=True,
            )
            return acc[:].rearrange("s (p u d) -> s u p d", u=2, d=2)

        def gate_side(e):
            relu_a = work.tile([P, 2, P, 2], F32, name="relu_a", bufs=E)
            nc.scalar.activation(relu_a[:], first_layer(e % 2, "a", w1, s1, e), RELU)
            return relu_a

        def value_side(e):
            return first_layer((2, 3, 7, 4, 2, 3)[e], "b", w3, s3, e)

        def hidden(relu_a, b):
            h = work.tile([P, 2, P, 2], BF16, name="h", bufs=E)
            nc.vector.tensor_tensor(h[:], b, relu_a[:], MULT)
            return h

        h_grouped = keep.tile([P, S * 4], BF16, name="h_grouped", align_bytes=64)

        def turn(dst, src, start=True, stop=True):
            nc.tensor.matmul(dst, src, ident[:], start=start, stop=stop, is_transpose=True)

        def turn_hidden(b, lo, hi, copy):
            turned = bank(b, "turned%d" % lo)
            for e in range(lo, hi):
                pairs = hs[e][:].rearrange("s u p d -> s (u p d)").bitcast(F32)
                for u in range(2):
                    at = (2 * (e - lo) + u) * C
                    turn(turned[:, at : at + C], pairs[:, u * P : (u + 1) * P])
            copy(
                h_grouped[:, lo * 4 * C : hi * 4 * C].bitcast(F32).rearrange("p (e s u) -> p e s u", u=2, s=C),
                turned[:, : (hi - lo) * 2 * C].rearrange("p (e u s) -> p e s u", u=2, s=C),
            )

        def quantise_hidden(lo, hi):
            cols = slice(lo * C, hi * C)
            nc.vector.quantize_mx(
                out=h_words[:, cols].bitcast(FP8X4), scales=h_scales[:, cols], in_=h_grouped[:, lo * 4 * C : hi * 4 * C]
            )

        def second_layer(b, nb, lo, hi, copy=nc.scalar.copy):
            acc = bank(b, "y%d_%d" % (nb, lo))
            for e in range(lo, hi):
                cols = slice(e * C, (e + 1) * C)
                nc.tensor.matmul_mx(
                    out=acc[:, (e - lo) * C : (e - lo + 1) * C],
                    lhsT=w2[:, e, nb * 2 * P : (nb + 1) * 2 * P].bitcast(FP4X4),
                    lhsT_scale=s2[:, e, nb * P : (nb + 1) * P],
                    rhs=h_words[:, cols].bitcast(FP8X4),
                    rhs_scale=h_scales[:, cols],
                    start=True,
                    stop=True,
                )
            copy(ysb[nb][:, lo * C : hi * C], acc[:, : (hi - lo) * C])

        for g in range(len(GATHER_GROUPS)):
            gather_tokens(g)
        relus, values, hs = {}, {}, {}
        for e in range(E):
            relus[e] = gate_side(e)
            if e < 4:
                values[e] = value_side(e)
        for e in (0, 1):
            hs[e] = hidden(relus[e], values[e])
            values[e + 4] = value_side(e + 4)
        turn_hidden(5, 0, 2, nc.scalar.copy)
        for e in (2, 3):
            hs[e] = hidden(relus[e], values[e])
        turn_hidden(6, 2, 4, nc.scalar.copy)
        for e in (4, 5):
            hs[e] = hidden(relus[e], values[e])
        turn_hidden(4, 4, 5, nc.vector.tensor_copy)
        turn_hidden(7, 5, 6, nc.scalar.copy)
        quantise_hidden(0, 2)
        quantise_hidden(2, 4)
        second_layer(0, 0, 0, 4)
        quantise_hidden(4, 5)
        quantise_hidden(5, 6)
        second_layer(5, 0, 4, 5, nc.vector.tensor_copy)
        second_layer(1, 0, 5, 6)
        for nb in range(1, NB):
            second_layer(6, nb, 2, 6)
            second_layer(1, nb, 0, 2)

        def gather_results(nb, r, lo, hi):
            t = work.tile([P, hi - lo], F32, name="prod%d" % r)
            part = pos[r][:, lo // 16 : hi // 16]
            nc.vector.tensor_tensor(t[:], ysb[nb][:].indirect(part), gates[nb][:, r, lo:hi], MULT)
            return t

        def combine_on_tensor(nb, lo, hi, pieces):
            sums = [bank(b, "sum%d_%d" % (nb, c0)) for b, back, c0, c1 in pieces]
            for r in range(TOP):
                t = gather_results(nb, r, lo, hi)
                for acc, (b, back, c0, c1) in zip(sums, pieces):
                    for c in range(c0, c1):
                        turn(
                            acc[:, (c - c0) * P : (c - c0 + 1) * P],
                            t[:, c * P : (c + 1) * P],
                            start=(r == 0 and c == c0),
                            stop=(r == TOP - 1 and c == c1 - 1),
                        )
            summed = work.tile([P, hi - lo], F32, name="summed")
            total = work.tile([P, hi - lo], F32, name="total")
            for acc, (b, back, c0, c1) in zip(sums, pieces):
                nc.scalar.copy(summed[:, c0 * P : c1 * P], acc[:, : (c1 - c0) * P])
            for b, back, c0, c1 in pieces:
                acc = bank(back, "back%d_%d" % (nb, c0))
                for c in range(c0, c1):
                    turn(acc[:, (c - c0) * P : (c - c0 + 1) * P], summed[:, c * P : (c + 1) * P])
                nc.scalar.copy(total[:, c0 * P : c1 * P], acc[:, : (c1 - c0) * P])
            nc.sync.dma_start(out[nb * P : (nb + 1) * P, lo:hi], total[:])

        def combine_on_vector(nb, lo, hi):
            first = gather_results(nb, 0, lo, hi)
            second = gather_results(nb, 1, lo, hi)
            third = gather_results(nb, 2, lo, hi)
            part = work.tile([P, hi - lo], F32, name="part")
            last = work.tile([P, hi - lo], F32, name="last")
            half = (hi - lo) // 2
            halves = (slice(0, half), slice(half, 2 * half))
            for cols in halves:
                nc.vector.tensor_tensor(part[:, cols], first[:, cols], second[:, cols], ADD)
            for cols in halves:
                nc.vector.tensor_tensor(last[:, cols], part[:, cols], third[:, cols], ADD)
                nc.sync.dma_start(out[nb * P : (nb + 1) * P, lo + cols.start : lo + cols.stop], last[:, cols])

        combine_on_tensor(0, 0, T, ((2, 4, 0, 3), (3, 5, 3, 5)))
        combine_on_tensor(1, 0, T, ((7, 4, 0, 3), (0, 5, 3, 5)))
        combine_on_tensor(2, 0, 256, ((2, 3, 0, 2),))
        combine_on_vector(2, 256, T)
